import numpy as np, ml_dtypes
CORES = [23,39,55,63,87,103,111,127,18,34,50,58,82,98,106,122]
N = 16
TOK, K = 256, 3
ROUTE = [[[4,12,15],[0,9,15],[4,6,15],[1,8,13],[6,7,8],[1,11,12],[3,6,11],[6,11,12],[3,7,9],[6,9,10],[2,8,13],[3,10,14],[5,6,12],[8,13,15],[4,5,7],[5,8,10],[7,11,13],[0,7,9],[3,11,14],[0,3,9],[10,12,13],[2,6,12],[3,12,15],[10,13,15],[5,11,14],[4,9,14],[4,12,14],[5,7,12],[10,11,15],[1,7,15],[9,11,12],[9,10,11],[5,7,10],[0,1,13],[5,7,12],[4,6,11],[5,7,8],[0,10,11],[4,8,15],[2,8,9],[9,10,15],[9,11,13],[7,10,13],[0,2,5],[0,7,9],[3,14,15],[0,2,9],[1,6,13],[5,9,10],[4,6,10],[2,10,11],[1,5,7],[6,7,10],[6,13,15],[2,3,4],[3,4,8],[4,7,8],[0,2,10],[8,13,15],[3,8,10],[5,7,15],[3,4,7],[4,8,10],[3,6,7],[1,3,12],[4,10,12],[1,3,13],[5,10,13],[8,11,12],[1,6,10],[5,6,11],[2,8,10],[0,3,6],[6,14,15],[1,5,6],[5,8,15],[8,9,14],[3,4,6],[0,5,9],[1,5,6],[6,10,13],[6,11,14],[5,6,10],[8,12,14],[5,7,10],[2,5,13],[1,11,12],[3,11,13],[2,7,14],[2,10,14],[4,6,11],[4,8,10],[2,5,10],[2,10,13],[0,4,6],[3,14,15],[2,11,15],[1,4,14],[2,3,12],[3,8,9],[12,14,15],[0,9,10],[1,12,15],[3,9,14],[5,6,7],[0,5,13],[2,11,12],[6,9,10],[2,3,15],[11,13,15],[4,7,11],[4,12,14],[2,12,15],[3,9,13],[1,7,11],[1,4,8],[1,2,13],[7,9,10],[0,1,14],[6,7,14],[1,3,8],[2,3,12],[0,13,14],[5,7,10],[4,5,12],[8,9,15],[3,4,7],[2,3,8],[2,3,7],[1,5,11],[6,7,15],[2,4,13],[5,6,14],[1,9,12],[0,3,6],[5,7,14],[1,2,4],[5,8,14],[0,11,13],[4,7,13],[3,5,15],[0,12,15],[3,7,10],[4,6,14],[0,3,9],[0,5,11],[4,5,14],[3,6,13],[0,3,10],[8,9,13],[4,7,11],[0,4,12],[2,4,14],[2,3,5],[1,3,7],[4,6,14],[3,6,15],[7,13,15],[2,5,8],[3,10,12],[1,14,15],[0,5,14],[1,11,13],[4,7,14],[3,13,14],[1,2,15],[1,2,10],[5,7,10],[0,10,15],[0,1,11],[2,5,6],[0,4,10],[7,8,15],[9,10,14],[3,5,7],[1,7,11],[1,2,4],[9,12,15],[3,11,15],[2,4,9],[0,8,12],[6,8,11],[7,13,15],[2,9,10],[1,7,8],[7,12,14],[2,8,11],[4,7,15],[7,9,10],[4,13,15],[1,6,8],[0,3,6],[1,11,12],[2,4,14],[3,5,6],[9,10,14],[2,5,10],[1,2,13],[6,8,12],[0,3,15],[1,4,12],[0,6,10],[4,8,10],[0,6,7],[3,11,12],[2,9,13],[9,11,14],[1,10,13],[0,1,8],[1,4,9],[1,3,5],[0,12,14],[0,3,15],[1,3,6],[1,9,15],[9,10,14],[0,6,14],[5,8,11],[7,11,14],[0,10,11],[4,10,15],[3,4,7],[3,6,10],[5,9,15],[4,8,15],[1,7,9],[3,7,13],[0,5,11],[8,12,13],[5,7,13],[0,9,11],[7,10,12],[4,5,7],[6,7,15],[3,9,14],[6,10,11],[2,4,15],[1,5,8],[2,10,14],[1,3,8],[2,9,13],[2,3,8],[2,3,5],[3,8,11],[9,11,14],[2,3,9],[2,11,13],[0,2,8],[3,10,14],[3,12,14],[0,5,11],[1,7,8],[4,9,11],[4,7,11],[10,11,15],[9,10,13]],[[7,9,11],[5,8,9],[8,9,10],[1,9,10],[2,6,7],[7,8,15],[4,6,10],[5,10,12],[6,7,15],[7,10,14],[1,2,8],[8,9,14],[6,12,13],[6,12,13],[3,9,13],[2,10,15],[6,9,13],[0,3,4],[4,5,7],[5,9,11],[1,9,13],[7,10,13],[1,5,7],[4,9,13],[0,2,9],[0,5,12],[6,12,14],[3,12,15],[1,4,6],[3,5,14],[1,8,12],[5,12,14],[7,13,14],[1,9,13],[1,5,12],[5,8,10],[0,5,9],[1,8,9],[4,6,14],[3,5,6],[3,12,15],[8,12,15],[0,4,8],[1,7,9],[0,11,14],[8,13,14],[1,7,10],[10,12,13],[7,13,15],[0,2,11],[7,9,14],[2,7,10],[7,8,14],[4,5,9],[2,12,15],[0,3,7],[3,4,5],[1,7,14],[1,2,12],[2,3,8],[0,12,15],[0,2,15],[0,3,9],[2,10,15],[2,12,15],[2,7,14],[1,4,14],[4,5,10],[2,12,15],[4,5,11],[7,9,13],[5,8,11],[3,8,11],[4,7,13],[0,11,12],[1,2,9],[2,6,15],[4,10,14],[4,5,8],[4,10,14],[2,7,13],[1,5,12],[5,13,15],[4,7,14],[1,3,7],[1,4,9],[2,12,15],[13,14,15],[7,8,13],[8,10,14],[7,9,10],[7,8,11],[4,13,14],[5,12,14],[10,11,12],[0,6,8],[2,3,9],[1,7,11],[9,11,15],[1,11,13],[1,5,15],[6,8,14],[6,8,11],[3,8,11],[0,3,13],[5,9,11],[0,6,14],[3,8,11],[3,4,12],[9,10,12],[1,5,6],[9,10,14],[10,11,13],[0,3,15],[2,12,15],[1,9,14],[0,10,12],[0,9,11],[0,8,12],[2,6,13],[8,11,12],[2,4,14],[2,9,13],[4,12,13],[1,3,11],[5,7,14],[2,6,10],[0,5,6],[2,5,9],[5,11,15],[2,8,15],[10,12,14],[1,2,12],[2,3,15],[3,6,7],[0,3,5],[10,12,14],[6,9,11],[3,4,10],[1,13,15],[1,3,12],[8,9,10],[0,3,9],[0,1,5],[0,2,12],[9,10,12],[1,10,14],[0,3,12],[0,4,14],[2,4,10],[3,6,9],[3,10,14],[5,11,15],[2,9,11],[1,2,7],[1,8,14],[0,6,13],[11,12,15],[3,8,12],[1,11,13],[2,3,6],[2,9,14],[4,5,13],[5,6,12],[0,2,6],[3,12,14],[0,5,13],[8,11,14],[2,4,5],[0,3,15],[2,13,14],[7,8,11],[12,13,14],[4,8,13],[7,14,15],[3,6,12],[8,11,15],[1,2,6],[0,10,14],[4,5,7],[6,12,15],[0,9,14],[6,11,14],[1,8,9],[2,7,12],[2,14,15],[1,2,11],[1,6,15],[3,14,15],[2,4,6],[3,7,15],[2,11,13],[5,7,11],[2,11,13],[1,4,13],[4,6,12],[5,8,15],[9,13,14],[1,3,13],[4,6,12],[2,5,14],[2,7,11],[10,11,13],[3,10,11],[0,1,14],[0,7,12],[7,9,13],[11,13,15],[1,4,12],[0,8,15],[5,7,14],[7,8,9],[2,6,14],[1,7,15],[2,13,14],[1,4,15],[4,10,15],[0,4,10],[1,5,15],[7,9,15],[6,7,14],[8,10,11],[8,9,13],[1,12,14],[3,9,10],[2,5,9],[1,3,9],[5,6,12],[0,4,13],[4,5,7],[7,8,15],[8,10,13],[6,8,9],[4,7,10],[4,5,15],[0,7,14],[3,8,15],[0,4,11],[5,6,13],[2,6,12],[5,8,14],[2,4,11],[7,10,11],[6,8,11],[8,9,12],[6,9,12],[9,11,12],[5,6,13],[5,8,14],[4,6,10],[4,9,15],[0,10,12],[3,8,14],[3,9,13],[0,2,9],[0,4,15]],[[6,11,12],[5,12,14],[5,12,13],[3,11,14],[2,12,15],[2,7,9],[5,13,15],[10,11,14],[1,5,15],[2,7,13],[3,4,7],[5,11,13],[3,8,15],[8,9,14],[0,2,13],[10,12,14],[9,10,15],[0,6,7],[0,2,9],[2,7,10],[1,2,13],[3,4,7],[5,6,7],[3,6,7],[3,4,9],[6,7,9],[0,4,5],[0,1,8],[1,14,15],[2,4,13],[8,9,13],[3,6,15],[2,9,12],[4,5,14],[8,12,15],[3,7,12],[1,4,6],[1,2,12],[0,6,10],[9,10,15],[2,5,8],[1,8,12],[0,8,11],[1,6,11],[2,5,12],[1,9,10],[2,4,10],[3,10,14],[5,8,9],[3,6,8],[1,9,13],[1,2,5],[7,10,13],[1,4,10],[0,2,14],[3,12,13],[0,9,10],[1,6,12],[1,9,15],[0,5,14],[5,11,15],[2,9,13],[7,9,15],[3,12,13],[4,10,12],[5,9,15],[0,2,7],[1,3,8],[5,12,15],[2,4,15],[12,13,14],[2,10,12],[3,9,13],[1,6,13],[8,9,10],[0,1,5],[2,3,13],[1,9,13],[4,6,7],[0,7,13],[4,7,10],[2,4,13],[10,14,15],[0,11,12],[7,9,15],[0,6,10],[1,10,12],[6,7,11],[0,11,12],[1,2,8],[4,12,14],[8,11,12],[4,8,14],[5,11,15],[0,6,15],[5,8,14],[4,5,13],[0,1,13],[0,11,13],[4,8,15],[0,2,12],[0,6,15],[3,5,7],[1,3,5],[1,5,14],[9,13,15],[8,13,14],[6,9,15],[10,12,14],[3,4,13],[4,6,10],[0,4,14],[4,9,10],[1,6,14],[2,9,10],[1,11,15],[0,3,4],[4,5,11],[0,2,8],[4,5,6],[5,9,14],[1,2,7],[4,8,15],[4,7,8],[0,3,14],[5,12,13],[0,13,15],[4,12,13],[1,4,14],[4,9,15],[2,9,15],[4,7,11],[0,1,2],[6,7,10],[2,6,14],[0,9,12],[0,10,11],[2,8,15],[1,11,13],[4,5,14],[3,12,13],[0,11,14],[1,5,13],[2,6,8],[3,9,13],[3,6,11],[0,9,14],[2,6,9],[0,8,10],[0,2,8],[10,11,12],[0,5,8],[0,10,12],[4,12,13],[1,2,15],[8,11,15],[2,3,6],[0,10,12],[0,5,9],[0,6,9],[1,3,10],[7,8,9],[2,5,8],[3,8,15],[5,9,12],[4,10,13],[0,13,15],[0,8,13],[0,3,7],[0,4,11],[0,6,10],[7,10,11],[5,11,14],[7,10,14],[1,2,12],[3,8,11],[6,10,11],[2,9,11],[1,5,9],[1,8,10],[1,9,15],[4,12,14],[5,12,13],[3,9,11],[3,5,14],[1,7,8],[4,7,11],[1,12,13],[6,8,10],[0,3,5],[8,10,14],[8,10,11],[4,5,9],[2,7,10],[6,12,14],[2,5,14],[0,3,11],[1,3,11],[4,11,14],[9,12,15],[1,7,13],[1,12,15],[3,5,8],[7,11,14],[0,12,13],[3,10,12],[4,7,9],[2,12,14],[9,11,13],[0,7,15],[2,4,12],[2,6,15],[1,2,10],[2,4,15],[1,12,13],[2,9,13],[8,9,11],[2,7,13],[2,9,10],[6,13,15],[0,1,5],[5,8,15],[3,11,15],[6,8,11],[1,2,9],[8,9,15],[5,8,12],[5,13,15],[12,14,15],[7,9,10],[5,9,12],[5,8,11],[3,6,12],[2,6,14],[0,3,6],[1,7,9],[2,4,14],[6,10,11],[1,5,14],[3,5,15],[2,5,13],[1,9,11],[0,4,15],[2,3,6],[0,4,9],[8,11,12],[0,4,8],[11,12,13],[1,14,15],[1,5,7],[6,7,9],[3,6,12],[9,12,14],[3,5,11],[7,10,13],[0,14,15]],[[1,12,14],[0,6,7],[6,7,12],[6,11,15],[3,10,12],[6,8,12],[6,8,12],[4,9,14],[0,1,2],[7,11,12],[4,9,12],[4,10,13],[1,5,11],[3,5,7],[5,11,14],[2,9,10],[4,9,15],[4,11,13],[4,7,9],[8,11,13],[4,12,14],[0,2,11],[0,1,3],[2,6,9],[1,10,12],[2,5,6],[6,14,15],[0,1,8],[5,11,13],[3,5,12],[2,9,10],[3,4,5],[1,6,13],[6,14,15],[4,5,8],[0,2,7],[1,3,8],[10,14,15],[3,7,10],[5,8,13],[3,7,11],[0,4,5],[1,4,12],[2,5,11],[9,10,15],[2,6,13],[4,9,11],[3,10,13],[3,4,13],[3,4,5],[6,7,9],[8,9,14],[1,3,15],[2,8,13],[2,14,15],[3,5,14],[4,6,10],[2,10,15],[0,6,9],[2,8,12],[4,13,14],[4,5,13],[7,9,15],[2,4,13],[2,5,12],[0,3,12],[10,11,15],[4,13,15],[0,2,11],[9,10,13],[0,1,4],[5,8,10],[2,8,14],[4,10,11],[4,10,15],[1,2,4],[4,11,13],[12,13,14],[3,5,6],[3,4,13],[0,9,11],[0,3,5],[3,4,11],[1,11,13],[3,9,12],[1,3,15],[4,5,14],[9,11,15],[1,9,13],[1,8,9],[2,7,13],[9,12,13],[8,9,14],[2,10,14],[4,6,11],[2,7,8],[6,14,15],[0,4,6],[5,11,12],[4,6,8],[0,8,12],[3,6,15],[8,12,14],[2,6,8],[0,10,14],[8,12,15],[0,7,14],[0,4,12],[2,4,8],[4,11,15],[1,11,15],[0,6,13],[0,1,4],[6,13,15],[3,7,8],[1,3,14],[4,8,10],[7,8,14],[2,4,7],[1,7,9],[0,5,13],[1,12,13],[1,4,12],[2,11,14],[8,10,15],[3,12,13],[2,3,9],[1,2,14],[4,5,11],[6,7,13],[0,12,15],[5,11,12],[3,9,11],[5,6,15],[1,4,6],[1,12,13],[0,12,15],[9,13,15],[0,6,10],[8,9,10],[5,12,14],[3,5,14],[2,13,15],[5,10,12],[7,10,12],[8,12,13],[2,7,8],[1,2,15],[3,5,7],[4,6,8],[4,8,12],[4,10,11],[2,9,10],[2,10,13],[1,7,12],[6,7,13],[4,10,14],[1,3,11],[6,9,12],[8,11,14],[0,5,15],[0,6,14],[6,8,10],[4,6,15],[6,9,12],[6,7,9],[1,2,11],[2,7,14],[1,7,8],[6,11,14],[6,7,14],[2,10,12],[1,8,9],[0,1,3],[7,12,14],[1,11,12],[3,12,14],[7,11,14],[2,7,8],[2,9,15],[0,9,10],[0,5,15],[1,8,11],[3,4,10],[3,6,13],[6,14,15],[1,4,6],[1,2,11],[1,12,15],[1,4,8],[3,6,14],[0,2,3],[2,10,12],[4,12,15],[5,8,9],[3,10,13],[5,12,13],[1,7,15],[7,9,14],[3,4,5],[0,3,14],[9,12,13],[1,2,5],[5,9,13],[2,10,14],[3,4,6],[0,5,12],[4,5,12],[3,4,14],[1,2,5],[3,9,11],[6,10,12],[1,6,13],[0,4,14],[8,11,15],[3,5,7],[5,7,14],[2,13,15],[3,11,12],[2,3,8],[1,10,13],[4,10,14],[9,12,15],[2,9,15],[0,5,13],[4,7,15],[4,13,14],[10,12,15],[3,6,12],[7,13,14],[5,9,13],[5,10,12],[0,2,5],[2,12,15],[9,10,13],[5,12,15],[3,7,9],[6,10,14],[1,13,15],[5,8,14],[1,7,9],[0,4,10],[5,11,15],[13,14,15],[3,7,12],[1,5,7],[0,5,12],[6,11,14],[8,9,10],[5,10,15],[1,6,13],[3,4,5],[1,2,10],[0,7,8],[0,9,12],[1,8,9]],[[0,1,3],[10,12,15],[2,6,11],[1,7,14],[2,3,5],[7,12,14],[2,7,13],[6,7,8],[0,8,9],[2,4,10],[2,9,15],[1,4,11],[9,10,14],[8,14,15],[1,2,5],[2,5,10],[0,13,15],[0,7,11],[1,8,15],[0,1,13],[4,11,13],[1,8,11],[0,3,9],[5,13,15],[7,11,12],[6,7,8],[0,3,6],[0,12,15],[10,11,14],[5,12,13],[0,10,12],[0,7,9],[11,13,14],[3,9,10],[0,7,10],[3,5,11],[1,12,14],[2,11,14],[2,10,12],[0,5,11],[5,10,15],[1,3,8],[2,4,7],[4,9,15],[1,5,9],[0,5,15],[2,10,12],[2,3,13],[6,12,14],[1,8,10],[4,7,11],[9,10,15],[6,14,15],[7,8,12],[2,5,15],[3,4,11],[7,11,12],[1,8,9],[0,6,15],[8,12,13],[0,11,14],[3,5,14],[0,4,7],[10,12,13],[0,7,9],[0,3,6],[0,1,9],[1,6,11],[0,4,11],[4,7,8],[4,7,8],[1,4,11],[1,3,4],[4,6,13],[1,4,10],[8,9,11],[3,7,15],[4,10,15],[0,10,11],[2,3,4],[11,12,13],[0,11,12],[3,6,9],[1,3,11],[7,11,14],[0,4,10],[3,6,13],[0,11,14],[2,3,14],[8,10,12],[0,2,10],[1,7,9],[0,12,15],[3,8,12],[6,8,10],[3,7,14],[0,4,5],[1,4,5],[1,12,13],[5,7,10],[3,6,11],[1,3,14],[10,13,14],[4,13,14],[12,14,15],[5,8,11],[3,4,13],[9,14,15],[4,5,15],[1,3,5],[5,7,13],[2,3,12],[1,12,13],[2,3,12],[3,4,10],[9,10,15],[2,9,12],[8,14,15],[2,4,8],[3,6,7],[0,8,9],[6,7,13],[1,2,8],[1,4,13],[2,6,7],[4,6,10],[5,8,15],[1,6,13],[8,10,14],[9,10,15],[4,14,15],[1,5,13],[5,6,13],[3,4,13],[4,7,8],[0,5,14],[2,4,7],[3,8,9],[2,7,15],[3,10,12],[0,1,12],[1,11,12],[4,5,14],[0,4,10],[4,8,11],[4,7,11],[2,7,11],[1,5,14],[5,7,9],[1,9,11],[0,2,14],[4,7,13],[2,6,7],[3,8,11],[0,8,15],[8,10,14],[4,6,9],[3,6,11],[3,8,15],[1,3,4],[4,6,13],[6,8,9],[5,10,14],[5,8,10],[1,10,14],[6,9,14],[1,11,12],[2,11,15],[1,5,14],[0,8,13],[8,11,15],[9,11,15],[0,3,4],[7,11,12],[6,11,13],[0,2,7],[1,6,12],[3,6,10],[4,9,10],[4,12,13],[5,8,15],[0,1,6],[6,8,13],[3,7,11],[7,11,12],[2,4,9],[7,8,14],[1,3,15],[0,2,9],[7,8,12],[5,8,10],[6,8,14],[0,1,15],[3,5,10],[3,8,11],[3,4,12],[3,5,6],[2,6,12],[5,8,13],[0,1,2],[5,6,10],[3,10,13],[6,10,13],[1,4,8],[8,11,15],[7,10,15],[9,11,13],[2,6,11],[1,5,10],[1,2,6],[4,9,14],[1,4,15],[4,7,8],[3,12,15],[0,11,12],[2,4,5],[7,8,14],[1,6,15],[1,14,15],[3,6,10],[3,10,12],[8,11,14],[0,5,7],[1,6,9],[7,10,15],[3,8,12],[9,10,15],[1,2,15],[8,13,14],[5,6,9],[2,14,15],[4,5,14],[5,12,14],[6,8,13],[2,3,13],[2,11,12],[2,11,13],[3,4,5],[1,10,15],[6,12,14],[6,11,15],[7,12,15],[2,9,11],[1,6,10],[1,3,9],[0,6,12],[2,4,5],[2,5,6],[0,10,12],[5,6,9],[0,7,10],[0,3,6],[3,12,15],[0,3,13],[3,8,9],[0,2,13]],[[1,2,4],[0,6,15],[0,8,10],[2,10,11],[0,2,6],[0,7,10],[2,4,9],[1,9,14],[6,14,15],[5,10,14],[7,12,15],[3,4,10],[0,10,11],[8,10,13],[1,2,10],[9,13,15],[0,3,15],[3,8,11],[7,13,14],[1,6,15],[1,6,11],[12,14,15],[1,8,9],[0,3,6],[2,9,13],[1,2,5],[1,3,14],[4,10,14],[0,4,7],[2,5,15],[2,5,10],[5,14,15],[6,8,9],[3,10,12],[3,5,9],[1,2,8],[1,7,14],[5,6,15],[1,6,14],[4,6,7],[2,4,14],[1,7,15],[0,3,13],[0,2,10],[5,7,11],[5,7,8],[4,7,8],[3,10,13],[2,3,12],[2,8,10],[9,13,15],[8,11,13],[5,10,13],[5,9,15],[0,13,14],[8,12,14],[2,4,15],[7,11,15],[7,9,15],[8,9,14],[10,14,15],[1,4,8],[2,7,13],[0,4,6],[0,2,6],[3,4,7],[7,8,13],[1,2,5],[3,7,8],[6,12,13],[7,12,14],[2,6,13],[1,6,7],[3,9,12],[0,10,13],[0,5,12],[1,6,8],[10,12,14],[5,7,15],[3,13,15],[5,9,10],[1,6,9],[4,8,9],[3,7,15],[4,11,14],[6,11,15],[0,4,14],[4,5,12],[3,4,14],[0,8,13],[0,5,11],[0,7,10],[4,7,8],[7,8,12],[0,1,6],[7,12,14],[3,4,13],[3,9,15],[0,9,11],[8,10,13],[11,12,15],[6,11,14],[1,6,14],[1,11,13],[0,3,10],[1,7,8],[4,9,11],[2,9,12],[6,7,8],[0,6,10],[1,10,11],[6,8,15],[7,11,14],[2,10,15],[6,12,13],[4,9,12],[0,10,15],[0,2,14],[9,10,13],[5,8,9],[5,8,11],[0,3,11],[4,7,9],[3,8,13],[2,8,9],[3,12,13],[0,1,3],[3,7,12],[0,6,14],[8,10,12],[10,12,15],[2,7,8],[7,12,14],[1,6,12],[9,12,14],[0,8,13],[10,13,14],[2,7,8],[0,3,4],[4,9,15],[1,12,13],[5,9,10],[8,12,15],[1,7,10],[4,10,13],[4,10,11],[5,7,8],[1,9,15],[1,6,13],[9,10,12],[0,5,15],[3,7,15],[0,3,15],[5,8,11],[5,6,8],[4,5,9],[0,3,4],[3,10,13],[10,11,12],[4,7,10],[1,6,10],[2,7,11],[4,7,12],[3,12,15],[1,5,11],[4,14,15],[11,13,14],[8,12,15],[1,4,5],[3,11,13],[3,12,13],[2,9,12],[2,8,15],[1,2,12],[3,8,12],[6,10,11],[8,11,15],[1,5,15],[5,11,12],[6,10,14],[1,8,14],[5,7,8],[1,2,14],[0,7,10],[1,6,14],[2,6,8],[1,6,9],[8,9,14],[0,1,10],[6,7,12],[0,8,12],[6,9,12],[0,5,14],[3,10,13],[6,13,15],[5,7,13],[2,9,10],[3,8,9],[12,13,15],[2,6,10],[4,10,12],[9,11,15],[2,4,6],[3,8,9],[2,9,10],[3,5,14],[1,8,14],[0,5,8],[0,9,15],[2,11,12],[2,11,14],[0,10,11],[0,2,12],[7,8,12],[4,5,11],[5,8,11],[2,3,5],[1,9,15],[2,4,6],[4,10,15],[6,7,15],[2,3,12],[1,3,9],[0,2,8],[0,8,15],[1,5,9],[0,9,13],[11,14,15],[1,7,15],[2,6,11],[2,4,14],[7,9,12],[9,10,14],[4,6,9],[0,4,5],[0,2,5],[3,8,12],[1,7,9],[1,3,4],[11,12,14],[4,5,15],[1,3,10],[0,2,12],[2,8,15],[1,2,9],[6,9,12],[4,8,12],[0,8,11],[3,5,12],[4,6,10],[5,12,13],[1,3,9],[8,10,14],[4,5,10],[1,6,8],[2,6,7]],[[7,9,12],[3,6,9],[1,10,11],[6,10,13],[8,10,15],[0,6,10],[5,12,14],[2,7,15],[4,13,14],[3,7,9],[4,7,13],[3,13,14],[1,2,4],[5,10,12],[4,6,11],[1,12,14],[8,9,11],[3,4,11],[0,1,13],[4,11,15],[3,5,15],[0,7,11],[4,9,10],[9,11,15],[0,8,10],[2,6,15],[2,5,13],[4,9,12],[2,6,12],[4,11,13],[1,13,15],[3,5,14],[3,4,5],[1,11,13],[1,4,5],[13,14,15],[3,8,11],[8,13,14],[5,8,14],[3,11,12],[6,13,14],[6,9,12],[4,5,15],[6,8,12],[3,12,13],[3,8,10],[2,3,15],[8,13,14],[1,9,11],[5,10,14],[3,7,15],[2,5,12],[12,14,15],[5,9,11],[11,14,15],[10,14,15],[5,8,11],[4,10,12],[3,4,8],[5,7,12],[7,13,14],[2,9,11],[2,4,14],[2,3,9],[8,10,13],[4,12,13],[2,4,6],[1,7,13],[0,11,14],[3,9,15],[4,5,8],[3,8,13],[0,3,6],[3,4,9],[0,4,15],[4,8,10],[4,7,11],[5,7,9],[1,13,14],[1,10,11],[4,7,13],[5,8,11],[1,8,10],[4,7,13],[6,10,15],[1,9,11],[3,8,12],[1,4,12],[2,8,11],[10,11,13],[9,10,11],[10,12,13],[0,12,14],[2,4,6],[1,5,9],[4,9,12],[0,1,3],[5,7,13],[1,6,15],[2,6,10],[2,8,9],[4,11,14],[1,2,10],[1,5,9],[3,6,12],[10,11,14],[3,4,6],[3,12,14],[5,12,15],[7,8,15],[6,9,15],[0,10,11],[0,8,12],[0,7,12],[1,3,13],[3,5,7],[0,3,11],[11,14,15],[7,11,12],[9,11,13],[3,13,14],[2,10,14],[1,2,14],[6,11,14],[3,7,8],[2,3,11],[0,1,10],[0,1,9],[4,12,13],[0,6,9],[4,5,10],[6,7,8],[1,9,13],[2,3,5],[1,2,5],[4,7,13],[6,13,15],[4,6,14],[3,4,11],[11,12,13],[0,1,6],[5,13,15],[1,3,10],[13,14,15],[2,12,15],[4,5,14],[5,8,12],[0,1,5],[2,6,12],[9,12,13],[9,10,13],[1,8,11],[4,9,14],[3,6,8],[0,14,15],[0,1,15],[0,8,9],[0,6,9],[4,6,10],[0,10,14],[6,10,14],[2,7,12],[9,12,13],[4,11,15],[4,7,14],[0,6,8],[4,5,12],[6,9,14],[2,4,6],[0,12,14],[4,11,13],[5,9,11],[5,10,13],[0,2,9],[1,5,15],[4,8,15],[2,5,15],[1,4,13],[1,4,11],[0,5,7],[3,5,14],[0,3,6],[0,1,7],[6,10,13],[6,9,15],[7,12,13],[1,2,12],[8,13,14],[0,9,11],[3,6,13],[1,2,14],[6,10,11],[1,4,13],[1,4,14],[0,14,15],[3,14,15],[2,6,10],[5,6,15],[6,12,13],[5,10,12],[2,5,10],[1,8,13],[2,3,6],[8,10,11],[3,6,10],[3,6,8],[0,10,14],[2,7,11],[0,2,7],[3,7,13],[8,13,15],[4,9,14],[3,6,13],[0,1,9],[1,9,14],[0,1,6],[1,9,15],[2,5,13],[9,12,14],[7,8,11],[8,13,15],[3,4,9],[2,9,11],[10,12,14],[3,5,15],[9,12,13],[5,11,15],[6,13,15],[11,12,13],[5,6,8],[6,8,12],[10,13,14],[6,9,10],[3,6,11],[0,8,11],[7,10,15],[8,12,13],[5,7,11],[9,11,13],[3,11,12],[2,9,13],[2,8,14],[0,6,9],[0,7,14],[1,8,13],[7,12,15],[8,9,12],[2,11,15],[4,6,15],[4,9,14],[2,13,15],[11,12,15],[0,10,14],[4,7,13],[0,11,13],[2,5,10]],[[0,8,12],[3,9,13],[0,6,9],[2,7,15],[0,8,15],[0,2,4],[8,9,13],[5,6,12],[6,8,13],[5,10,12],[1,11,13],[4,12,14],[2,6,14],[5,6,11],[2,12,14],[3,6,15],[5,7,15],[8,11,13],[2,9,11],[0,2,5],[1,7,13],[6,7,15],[2,7,11],[3,6,7],[7,11,13],[3,13,14],[0,1,9],[6,8,13],[7,10,15],[0,7,12],[6,13,14],[4,5,13],[0,10,15],[0,5,7],[4,12,15],[1,10,13],[1,4,15],[4,5,6],[2,3,6],[0,2,11],[6,7,15],[9,13,15],[0,1,13],[5,10,13],[1,9,11],[0,6,14],[1,11,12],[3,5,6],[6,8,12],[3,5,11],[1,5,12],[0,9,11],[0,10,11],[3,5,7],[2,6,13],[1,6,15],[1,7,14],[4,9,12],[0,1,6],[4,7,14],[2,8,13],[2,7,14],[6,11,13],[0,8,13],[7,9,15],[11,12,15],[5,6,13],[0,7,12],[4,8,12],[5,6,15],[6,7,8],[4,11,12],[1,5,9],[3,4,13],[7,10,15],[0,3,13],[3,11,14],[3,6,10],[6,9,15],[0,8,10],[0,5,7],[2,5,8],[1,2,12],[5,6,12],[0,6,7],[0,4,11],[8,10,14],[1,3,15],[3,5,6],[1,6,13],[0,11,13],[3,5,15],[0,2,8],[3,12,15],[2,3,7],[1,4,13],[6,11,13],[2,10,13],[1,2,3],[2,3,5],[0,9,14],[8,11,12],[2,4,15],[2,6,14],[2,9,13],[2,6,11],[6,10,13],[1,2,5],[11,12,14],[9,13,14],[8,12,15],[0,4,14],[0,5,14],[0,8,13],[0,1,3],[1,3,10],[2,12,15],[2,9,11],[2,3,15],[1,9,15],[3,4,11],[3,5,15],[4,9,10],[3,5,13],[2,4,15],[1,3,12],[7,9,13],[0,2,10],[1,5,10],[0,3,15],[2,6,7],[3,5,15],[7,13,14],[1,14,15],[3,4,9],[0,1,12],[1,10,11],[5,10,14],[2,5,10],[4,7,12],[2,8,14],[2,6,7],[1,13,14],[7,11,13],[3,5,7],[2,10,13],[1,2,10],[7,10,14],[3,4,6],[3,4,10],[0,3,9],[0,1,6],[9,12,14],[4,7,12],[10,11,15],[2,5,8],[4,7,13],[1,2,8],[0,10,12],[0,2,6],[5,7,9],[2,4,14],[1,5,7],[7,9,12],[4,5,6],[1,11,12],[0,4,12],[1,7,12],[5,10,11],[5,12,14],[0,3,9],[6,7,9],[1,8,11],[8,9,15],[1,10,11],[7,12,14],[1,11,15],[0,1,5],[2,10,14],[4,9,14],[2,5,12],[3,11,14],[5,7,8],[1,8,10],[0,13,15],[0,1,12],[4,7,10],[0,5,9],[0,13,15],[3,8,9],[2,4,9],[9,12,14],[6,10,15],[2,5,9],[0,1,3],[3,5,6],[5,10,15],[0,2,6],[5,10,14],[1,3,13],[12,13,14],[5,9,14],[0,8,11],[0,8,13],[4,7,8],[2,7,11],[0,4,8],[0,6,9],[0,9,15],[6,8,15],[1,10,15],[0,5,12],[1,3,10],[1,12,14],[4,6,14],[0,11,15],[1,10,12],[5,7,12],[1,6,15],[6,7,8],[1,5,8],[4,8,12],[5,7,15],[6,9,10],[3,4,6],[3,5,10],[1,5,10],[2,6,9],[8,11,15],[1,9,11],[5,13,15],[1,3,14],[1,11,12],[4,10,13],[9,12,14],[3,11,12],[0,4,6],[2,6,14],[0,1,14],[2,5,7],[3,6,12],[0,1,11],[1,9,14],[1,5,11],[10,12,14],[0,3,4],[4,8,13],[4,5,6],[2,7,11],[6,7,14],[2,6,11],[6,7,12],[3,13,15],[5,6,10],[6,10,15],[0,6,14]],[[4,9,13],[9,12,14],[6,7,15],[0,9,14],[1,5,13],[7,10,14],[9,10,14],[1,2,5],[7,12,15],[9,10,12],[6,7,12],[2,6,15],[1,2,4],[1,5,8],[7,14,15],[0,3,10],[0,3,7],[6,9,12],[5,9,10],[5,9,13],[0,8,13],[5,9,13],[3,5,7],[1,5,9],[2,10,14],[2,13,15],[5,9,12],[9,11,15],[2,12,13],[3,4,15],[3,11,15],[2,6,15],[3,7,12],[1,2,7],[1,4,9],[4,11,12],[1,7,13],[7,14,15],[9,12,14],[6,7,12],[2,3,8],[1,7,11],[0,4,13],[3,9,13],[0,10,11],[3,4,9],[7,8,12],[4,5,10],[9,13,14],[4,10,14],[0,1,6],[2,3,11],[5,13,14],[0,5,7],[0,10,14],[1,7,10],[4,10,14],[5,6,10],[2,3,6],[4,8,13],[9,14,15],[4,10,12],[4,10,14],[5,8,15],[0,5,10],[1,4,10],[0,11,13],[2,7,10],[8,9,13],[0,2,3],[3,9,15],[5,8,9],[3,4,6],[2,6,11],[3,7,13],[1,2,6],[6,10,12],[0,3,6],[2,3,12],[8,11,13],[2,7,8],[0,10,11],[4,10,13],[3,14,15],[1,14,15],[7,8,10],[4,6,13],[0,2,4],[0,9,13],[3,4,5],[6,7,10],[0,7,15],[0,9,13],[3,8,15],[2,11,14],[2,6,12],[3,8,15],[8,10,11],[0,8,14],[4,6,7],[0,4,14],[5,11,13],[4,9,15],[4,6,7],[11,12,15],[1,7,9],[4,5,7],[2,7,15],[2,9,13],[0,4,14],[3,10,13],[6,8,13],[0,13,15],[4,5,11],[1,9,11],[0,1,6],[1,7,14],[4,7,13],[6,7,14],[1,10,13],[2,7,8],[3,5,14],[0,2,15],[5,9,12],[8,11,13],[4,10,11],[1,4,6],[1,5,11],[2,3,8],[6,9,11],[5,12,14],[7,10,15],[0,4,6],[5,8,9],[0,12,13],[4,13,14],[3,7,8],[0,7,12],[2,3,8],[5,8,10],[3,8,9],[8,12,14],[7,12,13],[4,10,14],[3,5,13],[5,7,15],[3,8,12],[3,11,14],[7,12,15],[2,3,9],[1,5,10],[9,11,14],[5,8,15],[3,9,12],[4,5,8],[6,12,15],[7,8,15],[8,9,12],[5,8,12],[2,9,13],[11,13,15],[1,2,6],[0,5,12],[3,10,13],[2,10,13],[4,6,13],[0,1,4],[6,7,11],[0,3,8],[5,7,13],[4,7,10],[9,11,13],[5,6,7],[0,10,11],[6,8,13],[8,11,13],[4,7,12],[3,10,12],[2,7,11],[7,8,9],[3,10,13],[0,10,14],[10,14,15],[1,2,9],[0,10,14],[0,2,6],[0,12,14],[0,4,6],[1,5,9],[1,9,13],[6,8,12],[10,13,14],[3,7,9],[0,5,9],[5,12,15],[4,6,12],[2,7,8],[1,11,12],[2,5,6],[1,6,9],[1,6,15],[2,3,13],[10,11,12],[3,4,14],[2,14,15],[2,4,10],[5,6,14],[2,4,15],[3,10,12],[3,4,15],[7,8,9],[5,10,11],[3,7,8],[4,6,14],[1,5,9],[1,3,13],[1,9,10],[3,9,13],[5,6,7],[2,5,15],[0,8,12],[11,12,14],[3,9,15],[5,6,14],[7,9,10],[2,5,10],[4,5,13],[0,5,12],[8,11,13],[4,13,15],[0,4,12],[2,3,5],[1,9,13],[0,8,15],[0,13,15],[5,10,13],[0,8,13],[0,4,5],[1,6,10],[2,5,13],[0,11,14],[4,9,10],[1,7,10],[5,11,14],[2,9,12],[5,8,9],[3,14,15],[0,1,11],[1,6,12],[6,7,13],[1,11,12],[0,12,15],[0,1,6],[4,8,12],[8,11,14],[7,8,10]],[[10,11,14],[4,8,10],[12,13,15],[0,3,14],[0,7,11],[3,10,14],[0,7,10],[2,5,14],[3,9,15],[3,11,13],[9,12,14],[1,8,9],[3,12,13],[1,4,15],[1,7,11],[6,7,13],[1,2,15],[0,6,15],[4,10,11],[1,7,12],[6,9,12],[8,11,14],[9,11,15],[1,3,8],[2,3,5],[2,11,14],[0,4,12],[1,8,9],[3,9,11],[1,8,15],[1,5,13],[5,13,15],[5,9,10],[0,3,15],[1,2,13],[0,4,15],[1,3,8],[0,2,15],[5,6,13],[0,3,11],[3,12,15],[5,8,14],[6,11,14],[5,13,15],[3,11,14],[3,4,13],[0,4,14],[2,4,15],[1,12,14],[2,6,14],[9,12,13],[0,1,7],[8,9,15],[1,5,6],[3,12,13],[0,13,15],[2,4,5],[2,6,15],[7,9,14],[3,4,9],[9,12,15],[10,13,14],[0,8,11],[5,7,13],[8,9,11],[1,8,11],[1,11,15],[3,6,14],[0,2,10],[2,4,12],[7,12,15],[1,9,11],[8,13,15],[0,3,5],[0,1,12],[5,6,14],[2,8,12],[1,3,7],[1,5,9],[8,10,14],[0,5,8],[1,6,10],[6,9,15],[7,12,15],[7,9,12],[2,4,7],[2,8,10],[1,9,13],[7,11,14],[1,3,4],[3,8,10],[12,13,14],[4,7,8],[4,6,9],[6,7,13],[1,4,6],[2,7,14],[0,8,9],[3,10,11],[0,12,15],[1,4,10],[3,12,15],[2,3,8],[5,7,10],[0,1,15],[0,1,9],[5,6,8],[1,7,11],[2,5,11],[6,8,9],[1,5,6],[6,8,10],[6,9,12],[7,11,12],[6,10,12],[6,7,12],[4,7,14],[3,4,13],[6,7,10],[5,8,14],[0,1,4],[0,2,5],[3,6,11],[0,6,8],[1,6,13],[1,8,15],[1,3,13],[4,5,7],[5,8,14],[1,8,10],[5,7,15],[4,11,12],[1,3,10],[3,13,14],[0,5,6],[5,11,12],[3,14,15],[3,8,15],[0,5,14],[0,1,15],[3,13,14],[0,6,10],[3,10,11],[1,4,12],[12,13,14],[0,5,11],[0,8,9],[4,5,11],[0,3,4],[1,2,3],[2,5,7],[2,6,10],[0,3,14],[3,7,12],[11,12,14],[6,8,11],[2,12,13],[6,7,11],[7,8,13],[9,13,15],[9,13,14],[10,11,13],[7,10,14],[2,9,13],[0,10,15],[3,12,13],[3,7,14],[5,9,10],[0,1,6],[4,7,8],[0,2,11],[1,2,3],[4,11,13],[2,5,11],[7,11,14],[3,8,15],[3,6,15],[11,13,14],[1,5,11],[1,10,13],[11,13,15],[7,9,11],[1,2,5],[1,10,12],[0,11,14],[4,13,15],[5,9,11],[2,6,9],[2,11,13],[0,1,11],[3,6,9],[0,5,6],[1,9,13],[5,10,11],[5,8,10],[2,11,15],[3,5,6],[4,8,15],[1,7,11],[0,3,14],[9,10,13],[0,10,13],[6,14,15],[5,14,15],[5,9,11],[9,10,14],[4,11,13],[0,4,13],[2,8,11],[1,6,7],[6,8,13],[1,7,13],[1,12,15],[5,10,11],[0,9,13],[0,14,15],[11,14,15],[2,11,13],[0,4,5],[1,5,15],[11,13,15],[0,6,11],[2,9,11],[8,10,12],[1,4,15],[9,12,13],[6,11,15],[10,12,13],[3,10,11],[3,6,9],[0,5,10],[7,13,15],[1,7,8],[2,9,15],[4,7,12],[1,4,8],[3,7,12],[0,7,15],[2,5,6],[2,14,15],[1,3,15],[0,3,4],[7,8,15],[3,6,9],[0,3,6],[6,8,15],[0,5,6],[3,10,11],[5,6,9],[9,10,11],[2,4,10],[0,5,15],[3,4,9],[5,9,15],[1,8,11],[6,10,14]],[[0,8,12],[5,9,14],[4,11,14],[4,9,14],[11,14,15],[0,7,15],[3,9,15],[0,2,3],[6,10,13],[1,7,13],[2,3,4],[6,7,11],[1,5,14],[0,11,13],[5,11,13],[9,10,12],[0,3,5],[2,3,12],[1,8,10],[5,11,13],[9,14,15],[2,3,10],[2,9,13],[5,7,14],[7,12,13],[10,13,15],[2,3,13],[2,7,11],[8,9,13],[9,12,13],[2,3,14],[7,8,11],[4,5,12],[3,7,14],[0,9,12],[0,8,15],[6,9,13],[5,6,8],[0,4,12],[1,4,8],[6,7,11],[2,8,14],[1,2,9],[2,8,13],[3,7,8],[4,9,12],[0,5,6],[1,6,9],[2,5,12],[0,13,14],[0,4,14],[2,3,15],[0,1,5],[7,12,14],[1,5,7],[4,8,15],[0,13,14],[2,5,6],[4,5,10],[0,1,10],[9,10,11],[2,4,12],[1,6,9],[0,1,9],[4,12,15],[0,4,15],[1,12,13],[1,6,7],[3,12,15],[0,2,14],[8,10,11],[3,12,13],[1,3,8],[2,9,14],[0,1,2],[4,7,10],[2,3,14],[1,9,15],[1,5,10],[0,9,13],[4,10,15],[3,6,13],[5,6,10],[8,12,14],[0,3,6],[0,8,9],[0,2,13],[3,7,15],[2,8,14],[3,7,13],[1,11,14],[5,6,7],[1,5,12],[10,11,15],[3,9,14],[7,13,14],[3,5,15],[2,12,14],[7,9,11],[1,4,7],[7,10,14],[2,4,8],[7,10,13],[5,6,7],[6,11,12],[1,5,8],[9,10,11],[0,4,10],[0,3,15],[5,8,11],[2,12,14],[7,9,13],[1,4,15],[0,5,11],[2,3,9],[4,8,15],[1,2,9],[1,7,12],[1,4,15],[10,12,15],[3,10,14],[0,4,15],[6,8,11],[2,5,12],[1,5,14],[3,9,11],[4,9,13],[3,4,5],[7,12,13],[4,6,11],[4,9,14],[5,7,12],[3,4,6],[3,10,15],[3,9,10],[1,10,12],[0,1,2],[1,8,12],[4,5,10],[2,5,7],[2,5,15],[0,4,10],[1,5,10],[6,10,12],[2,7,11],[1,4,7],[2,8,10],[0,3,10],[4,7,13],[4,7,12],[9,10,15],[4,7,11],[3,5,9],[3,10,15],[0,6,15],[0,3,6],[9,10,15],[8,9,15],[8,11,15],[2,3,15],[2,9,10],[3,6,8],[3,9,13],[0,2,4],[5,7,13],[12,14,15],[1,9,13],[1,5,11],[6,11,15],[0,3,14],[3,6,13],[6,12,14],[2,10,12],[9,10,14],[6,12,14],[8,9,10],[5,6,12],[7,10,11],[3,4,9],[1,6,13],[4,6,13],[8,13,14],[3,9,14],[10,12,15],[2,4,7],[4,9,13],[5,9,14],[2,12,13],[3,4,9],[1,11,12],[1,4,13],[6,8,11],[0,2,5],[6,7,13],[1,5,13],[1,2,6],[1,9,12],[1,3,12],[3,11,14],[1,5,7],[2,7,10],[0,4,7],[5,10,15],[1,6,15],[3,7,9],[2,3,6],[5,7,14],[7,9,10],[4,8,10],[8,13,15],[2,3,8],[0,8,14],[6,12,13],[0,3,11],[3,4,11],[0,4,5],[11,12,14],[0,3,4],[4,8,12],[1,7,13],[2,5,14],[8,10,13],[0,3,7],[8,10,11],[1,3,6],[3,7,10],[1,2,14],[4,6,13],[6,8,15],[3,8,9],[0,10,14],[5,9,13],[0,6,9],[0,2,3],[9,12,15],[13,14,15],[8,9,14],[2,6,12],[5,10,12],[1,7,15],[6,11,14],[7,8,12],[1,10,12],[6,8,14],[0,4,11],[1,10,11],[5,6,12],[1,2,15],[0,11,13],[6,9,10],[4,9,14],[1,2,11],[2,7,15],[0,4,11],[0,6,10],[4,8,9]],[[2,8,14],[0,3,12],[6,7,9],[0,4,13],[8,10,15],[8,14,15],[3,7,13],[6,7,10],[1,11,13],[0,13,14],[1,8,12],[12,14,15],[0,6,13],[9,10,11],[2,4,12],[9,10,14],[4,5,9],[9,13,14],[4,7,8],[2,13,14],[8,10,13],[4,7,9],[0,2,7],[2,3,13],[10,14,15],[6,8,14],[2,3,13],[2,12,14],[0,4,15],[8,11,14],[6,9,14],[1,4,6],[10,11,12],[4,11,12],[6,7,13],[6,8,9],[4,7,11],[6,9,14],[9,10,11],[1,7,15],[0,8,10],[8,12,15],[4,5,7],[1,7,12],[6,13,14],[1,5,7],[4,6,8],[0,5,10],[1,4,13],[0,11,15],[7,11,14],[0,5,8],[2,7,13],[5,6,10],[2,6,9],[8,10,12],[2,9,15],[9,11,15],[1,5,13],[9,13,14],[4,8,10],[8,10,13],[0,3,11],[1,4,10],[1,12,13],[1,5,6],[1,6,9],[2,8,12],[2,6,7],[0,3,14],[7,13,14],[0,1,13],[2,3,15],[0,7,11],[3,4,11],[5,11,12],[1,4,5],[11,14,15],[2,6,15],[1,7,13],[1,4,8],[1,6,9],[5,14,15],[7,9,15],[2,7,15],[11,14,15],[0,1,15],[4,7,15],[3,5,11],[1,3,12],[1,2,9],[7,8,12],[1,8,14],[7,12,15],[8,9,13],[0,7,9],[0,5,12],[1,4,6],[3,4,11],[5,6,7],[2,12,14],[2,8,13],[6,7,14],[1,11,12],[2,7,14],[2,6,15],[9,12,15],[0,8,10],[3,4,12],[3,4,11],[2,11,12],[0,10,14],[1,4,14],[7,12,14],[9,12,14],[8,9,12],[13,14,15],[3,7,15],[0,8,14],[9,12,14],[0,8,11],[1,8,15],[1,4,5],[0,4,7],[0,10,15],[7,8,9],[3,6,7],[1,8,14],[5,10,15],[6,7,9],[5,6,11],[2,7,14],[5,10,12],[1,7,11],[0,11,13],[2,4,5],[6,9,10],[6,11,13],[12,13,15],[0,2,10],[1,3,14],[3,13,15],[3,14,15],[2,12,14],[3,9,13],[0,7,9],[10,11,13],[3,4,11],[1,3,8],[6,8,12],[2,5,7],[6,10,13],[8,12,13],[4,5,8],[5,8,11],[2,6,12],[4,10,15],[1,11,12],[10,14,15],[9,10,11],[4,5,13],[4,10,11],[2,10,11],[2,6,9],[4,6,13],[1,5,15],[6,12,15],[2,13,15],[0,8,11],[1,2,6],[7,11,13],[2,11,13],[1,5,11],[0,1,5],[0,7,13],[1,2,9],[0,9,14],[1,4,7],[1,5,10],[1,7,9],[6,10,15],[2,11,12],[2,3,13],[0,5,8],[0,7,11],[1,4,13],[2,6,12],[4,8,10],[0,6,12],[1,5,14],[2,3,5],[8,9,10],[4,7,15],[1,5,8],[3,12,15],[3,4,9],[1,3,6],[1,9,12],[0,1,10],[4,6,8],[0,9,15],[3,7,14],[4,5,13],[10,12,15],[0,3,7],[6,7,9],[3,4,9],[1,11,13],[2,7,8],[5,6,13],[0,6,11],[1,4,12],[4,10,11],[0,9,12],[8,10,13],[0,11,13],[1,5,15],[0,2,4],[2,4,14],[5,9,10],[2,6,15],[1,2,5],[6,11,12],[1,11,15],[7,13,15],[1,4,10],[3,4,15],[6,14,15],[0,7,11],[8,12,13],[0,2,6],[4,13,14],[5,8,12],[3,7,8],[0,2,15],[0,1,8],[0,3,4],[8,10,11],[8,9,10],[2,5,13],[2,3,11],[0,1,11],[1,2,7],[10,12,15],[0,4,9],[3,7,8],[1,13,14],[1,8,12],[1,8,14],[7,10,15],[2,12,14],[6,9,14],[7,8,10],[5,7,11],[1,4,12],[0,1,6]],[[3,8,12],[0,11,13],[9,10,14],[1,9,13],[4,8,9],[1,8,9],[0,8,9],[7,11,12],[4,8,13],[11,12,13],[2,4,10],[2,9,10],[1,2,15],[4,10,11],[1,2,5],[7,14,15],[2,4,10],[6,8,15],[6,10,11],[2,8,10],[4,5,12],[7,9,12],[4,7,8],[10,13,14],[2,6,13],[12,13,14],[1,9,12],[10,12,15],[7,9,15],[3,9,14],[0,6,10],[3,10,15],[9,10,12],[2,5,13],[2,3,8],[1,3,14],[7,9,15],[2,10,12],[4,10,14],[0,2,13],[2,6,10],[1,11,14],[0,2,12],[0,9,11],[1,11,13],[0,2,5],[4,6,12],[1,4,11],[2,6,14],[3,5,7],[10,13,14],[5,7,11],[1,2,8],[4,5,8],[5,6,10],[2,8,9],[0,6,13],[4,7,8],[8,10,15],[5,12,13],[6,9,12],[3,9,14],[4,5,6],[1,5,9],[0,5,12],[0,11,12],[2,14,15],[6,9,10],[1,5,15],[6,13,15],[3,4,15],[3,4,7],[4,7,10],[3,4,15],[1,2,3],[4,8,9],[4,7,14],[3,6,11],[0,7,8],[0,5,12],[5,6,13],[1,2,7],[6,9,11],[4,9,14],[2,3,10],[5,9,13],[0,1,9],[0,4,6],[1,6,13],[8,11,14],[2,4,12],[5,7,9],[6,10,13],[1,3,8],[4,7,12],[3,13,15],[1,6,14],[0,2,4],[4,7,14],[5,6,13],[1,3,8],[3,10,13],[3,4,11],[4,10,14],[7,12,13],[0,7,14],[11,13,14],[0,13,15],[1,8,15],[0,12,14],[1,5,14],[7,9,13],[0,1,5],[4,6,7],[0,1,14],[0,1,5],[1,9,14],[6,10,13],[4,6,15],[0,3,5],[8,9,10],[6,14,15],[0,3,7],[3,9,15],[3,5,7],[0,13,14],[4,10,15],[2,3,8],[5,6,12],[1,10,15],[4,5,15],[5,7,12],[1,12,14],[0,4,14],[1,6,12],[11,12,14],[7,10,15],[4,13,15],[4,7,9],[3,12,14],[2,5,11],[6,7,10],[1,4,9],[1,5,12],[1,2,7],[5,9,12],[8,10,14],[7,10,12],[4,11,14],[8,14,15],[0,3,7],[1,6,12],[2,8,13],[0,1,14],[0,2,8],[3,6,7],[1,3,6],[3,6,8],[5,8,14],[0,2,6],[0,12,15],[0,1,11],[1,3,12],[2,8,13],[2,7,11],[2,13,14],[0,13,15],[3,6,13],[8,10,14],[6,9,11],[0,2,4],[4,6,9],[5,7,10],[7,8,14],[8,9,14],[4,7,12],[1,3,8],[3,5,10],[8,9,12],[5,14,15],[0,8,12],[2,7,15],[0,8,14],[2,10,15],[10,13,15],[3,5,6],[0,6,7],[2,5,13],[5,6,10],[1,6,7],[5,6,12],[2,5,12],[6,12,14],[0,1,7],[5,8,13],[0,4,14],[1,3,15],[7,9,14],[1,6,14],[3,5,7],[2,8,14],[6,12,13],[1,6,9],[5,7,10],[0,3,5],[5,8,11],[2,7,9],[6,9,10],[8,10,15],[3,4,10],[3,5,9],[0,1,10],[0,1,14],[0,2,6],[2,6,13],[0,2,13],[1,12,13],[4,10,14],[0,1,15],[0,3,13],[6,13,15],[0,3,5],[7,10,12],[5,13,14],[7,8,13],[0,1,10],[2,9,12],[6,8,13],[0,5,10],[2,3,6],[5,13,14],[1,9,10],[0,10,15],[0,3,11],[9,10,13],[3,7,8],[1,3,12],[3,5,9],[3,7,13],[6,9,15],[10,12,13],[4,11,15],[5,7,13],[2,7,12],[6,11,13],[5,9,13],[2,9,11],[4,8,15],[0,1,9],[1,4,15],[0,2,8],[5,9,14],[3,6,11],[3,6,11],[3,5,11],[0,1,3]],[[3,8,13],[1,5,7],[3,5,11],[3,6,11],[2,8,11],[7,12,13],[1,4,6],[7,12,14],[2,4,8],[9,13,15],[2,6,15],[6,13,15],[5,11,13],[1,6,15],[3,4,5],[1,2,11],[4,13,14],[6,7,15],[0,4,6],[9,10,11],[1,7,12],[1,4,8],[0,2,4],[5,12,14],[1,9,12],[3,4,5],[0,5,10],[0,3,7],[0,10,15],[4,5,6],[0,1,14],[0,10,11],[1,3,6],[2,5,8],[7,9,12],[4,9,11],[9,13,15],[3,4,10],[3,9,14],[5,6,11],[6,7,10],[0,9,15],[10,12,15],[3,9,13],[5,14,15],[11,12,15],[2,8,13],[1,2,12],[0,2,12],[12,13,14],[1,3,12],[8,11,14],[1,13,14],[0,6,12],[2,7,14],[3,10,12],[3,5,7],[2,3,10],[5,10,15],[4,6,8],[4,8,14],[5,6,7],[6,10,12],[4,9,10],[2,12,15],[10,12,15],[1,6,8],[3,4,9],[2,6,7],[6,8,9],[1,5,13],[4,9,14],[2,8,9],[0,13,14],[3,7,10],[3,6,9],[0,4,10],[3,4,8],[0,3,15],[7,8,14],[1,8,10],[1,10,12],[0,2,13],[0,2,11],[1,6,9],[3,4,11],[4,5,11],[2,14,15],[3,5,9],[0,3,11],[3,6,13],[2,6,10],[3,5,12],[0,8,14],[4,5,13],[6,8,13],[0,2,13],[5,9,12],[2,4,7],[2,4,10],[1,10,15],[0,4,7],[0,12,15],[0,3,9],[5,7,15],[1,4,5],[1,4,6],[4,8,13],[6,7,8],[5,11,12],[5,12,14],[0,4,12],[5,13,15],[0,13,15],[3,8,14],[4,8,13],[3,6,9],[5,9,12],[3,8,11],[3,6,11],[5,7,15],[1,2,4],[4,7,13],[0,1,4],[0,5,6],[0,13,14],[3,9,14],[1,10,14],[4,8,10],[1,2,8],[2,4,6],[5,12,13],[0,2,11],[0,6,15],[1,2,12],[5,8,11],[5,11,14],[12,13,15],[5,9,14],[0,5,13],[4,9,14],[0,9,10],[0,2,14],[7,8,14],[8,12,14],[3,13,15],[2,8,10],[0,12,15],[1,7,11],[0,2,6],[1,10,13],[5,6,10],[5,6,10],[10,13,14],[1,7,14],[2,12,13],[8,9,15],[2,3,13],[8,13,14],[4,7,14],[2,3,14],[0,3,13],[0,11,15],[6,8,12],[9,10,14],[7,8,12],[11,13,15],[3,12,14],[0,12,15],[2,10,14],[0,1,15],[7,9,12],[2,6,8],[1,11,15],[0,5,6],[0,1,15],[6,9,12],[4,8,13],[2,7,13],[2,8,15],[0,12,13],[0,2,7],[3,5,15],[7,9,11],[0,5,14],[2,4,7],[7,9,10],[1,4,15],[4,6,15],[2,7,11],[0,5,7],[2,3,11],[1,9,15],[0,7,11],[4,8,11],[1,13,14],[5,6,15],[3,7,10],[8,13,15],[2,9,14],[2,3,8],[7,12,13],[0,6,14],[1,9,15],[10,13,14],[4,7,8],[2,3,8],[3,8,14],[0,9,15],[1,3,6],[0,8,10],[5,9,12],[2,5,8],[1,10,12],[1,9,13],[6,11,14],[1,4,14],[3,4,10],[0,7,11],[7,13,15],[1,14,15],[5,6,7],[4,7,10],[2,4,13],[1,8,15],[0,8,11],[1,10,12],[1,3,6],[3,10,15],[2,4,14],[6,10,13],[2,9,11],[1,2,9],[1,5,10],[0,8,11],[2,13,14],[0,6,7],[3,12,13],[3,7,10],[5,6,7],[11,13,14],[1,7,14],[3,6,14],[2,4,9],[9,11,13],[9,10,13],[2,4,11],[0,2,4],[2,10,13],[6,9,11],[5,6,10],[1,4,15],[4,13,14],[3,6,13],[2,4,11],[0,4,10]],[[7,10,14],[9,12,15],[1,2,3],[0,13,14],[8,10,14],[3,6,9],[0,3,10],[0,4,14],[2,6,15],[3,5,12],[1,5,11],[6,11,14],[0,8,14],[1,5,8],[0,5,8],[1,4,8],[0,8,13],[0,2,15],[0,1,3],[5,11,15],[5,8,15],[12,14,15],[9,11,12],[1,4,5],[0,2,15],[0,10,15],[11,12,15],[7,14,15],[5,10,14],[1,2,4],[5,9,14],[9,10,15],[8,10,14],[7,8,11],[1,6,8],[2,6,11],[2,6,10],[3,8,10],[1,2,7],[4,11,14],[0,8,10],[1,3,4],[1,9,15],[1,4,14],[6,10,11],[0,3,12],[9,10,12],[1,5,15],[0,4,14],[6,9,10],[0,11,15],[5,7,15],[5,8,9],[0,2,10],[0,1,12],[7,8,11],[1,13,15],[7,9,10],[2,9,12],[8,10,15],[1,2,7],[4,7,11],[7,8,10],[3,7,12],[0,7,12],[7,8,13],[4,9,10],[9,13,15],[0,2,8],[1,2,10],[2,5,8],[3,9,14],[6,11,14],[4,12,15],[5,7,13],[10,13,15],[2,12,14],[1,3,6],[2,6,11],[6,8,15],[1,4,12],[1,5,8],[5,6,15],[3,10,12],[8,11,14],[0,5,15],[6,8,14],[8,13,15],[1,10,14],[1,4,13],[3,4,13],[6,8,9],[2,4,6],[0,8,13],[0,6,12],[4,8,12],[2,4,13],[0,3,10],[0,2,6],[2,13,14],[7,8,9],[0,6,11],[5,11,13],[9,11,15],[0,5,13],[3,9,15],[1,5,9],[4,7,8],[6,8,12],[5,9,13],[1,5,12],[1,9,14],[7,9,15],[3,11,14],[5,13,14],[0,11,12],[0,3,11],[4,5,14],[4,8,15],[9,10,13],[6,11,15],[5,12,14],[1,12,13],[6,8,11],[2,5,13],[8,11,13],[3,9,13],[6,7,10],[0,1,15],[9,12,13],[1,2,3],[1,6,15],[5,10,14],[5,10,12],[2,7,10],[9,13,15],[1,2,11],[6,9,13],[4,10,14],[1,4,14],[1,10,12],[5,12,13],[5,13,14],[1,9,10],[5,8,13],[2,4,13],[1,5,10],[0,5,10],[2,5,13],[4,7,13],[3,7,14],[9,12,13],[0,3,12],[3,6,10],[5,11,13],[4,10,11],[6,10,13],[0,5,8],[2,8,13],[2,3,5],[2,4,10],[1,10,14],[11,12,15],[1,13,14],[3,6,10],[3,9,11],[2,12,15],[10,13,14],[2,6,9],[10,12,15],[1,4,13],[2,6,15],[0,6,9],[11,14,15],[3,6,13],[4,12,13],[0,4,13],[0,4,5],[3,5,6],[0,12,14],[2,5,8],[3,8,14],[11,12,15],[0,6,8],[6,7,10],[11,13,14],[3,5,11],[2,5,10],[6,7,15],[3,10,11],[1,8,12],[0,3,10],[2,11,15],[1,6,8],[0,2,7],[6,9,14],[2,4,7],[2,10,15],[0,6,9],[4,11,13],[1,6,13],[0,7,11],[0,8,12],[9,10,11],[0,4,12],[1,13,15],[6,9,12],[3,6,7],[0,3,14],[0,6,8],[2,10,14],[1,5,13],[0,7,13],[2,9,10],[0,4,13],[7,8,15],[3,10,12],[7,8,9],[1,2,13],[3,7,12],[5,6,9],[9,10,14],[0,7,9],[0,4,15],[11,14,15],[7,8,15],[1,5,15],[0,4,14],[0,8,11],[1,5,9],[3,7,12],[4,5,7],[1,4,8],[10,11,12],[0,9,11],[2,3,15],[0,4,12],[6,7,11],[8,12,13],[0,13,14],[0,3,4],[0,4,15],[0,1,14],[2,6,12],[2,4,8],[6,9,10],[0,2,8],[0,2,15],[0,3,7],[5,11,15],[0,2,11],[0,6,15],[0,7,13],[9,11,13],[3,8,14],[3,9,11]],[[0,2,7],[7,9,12],[1,6,9],[4,7,14],[7,8,10],[2,7,12],[2,5,11],[3,6,13],[7,10,14],[2,3,6],[9,11,14],[0,1,10],[4,10,13],[3,5,10],[7,8,13],[2,8,10],[0,3,6],[3,13,14],[1,4,14],[1,6,11],[7,11,15],[5,8,12],[1,10,13],[1,3,15],[8,9,15],[2,4,7],[6,7,14],[7,13,14],[2,9,12],[3,11,13],[1,3,10],[2,4,10],[2,6,14],[9,10,14],[0,13,14],[2,11,15],[0,2,9],[0,6,8],[9,14,15],[2,5,8],[1,8,10],[11,13,15],[1,11,15],[12,14,15],[0,2,6],[2,5,10],[0,1,13],[2,5,6],[1,7,12],[5,6,14],[2,8,11],[4,6,7],[8,10,11],[1,3,10],[2,6,11],[9,10,15],[5,9,15],[7,9,15],[0,4,10],[1,9,12],[7,11,14],[1,2,3],[6,9,10],[6,10,14],[3,11,14],[8,9,13],[1,8,13],[2,9,12],[4,5,10],[0,4,15],[0,1,13],[4,14,15],[2,8,15],[3,11,14],[6,12,14],[2,5,15],[4,11,14],[0,4,15],[10,13,15],[6,11,13],[1,2,8],[2,4,12],[5,10,11],[8,9,12],[2,4,8],[0,7,10],[4,11,14],[3,10,14],[0,2,13],[2,10,14],[0,5,13],[3,4,12],[2,5,13],[0,10,12],[1,4,8],[0,10,12],[6,8,15],[2,4,7],[4,8,12],[1,3,9],[0,9,10],[2,12,15],[5,7,13],[2,9,14],[7,8,14],[3,5,8],[0,5,6],[2,7,14],[1,7,15],[0,3,6],[1,5,9],[4,7,15],[13,14,15],[3,5,11],[2,5,6],[4,11,14],[1,7,10],[4,7,15],[6,8,10],[2,3,5],[8,9,10],[3,4,11],[6,7,11],[6,10,11],[0,8,13],[3,8,11],[2,5,9],[0,1,13],[4,5,8],[6,7,9],[10,13,14],[0,8,15],[2,4,8],[0,2,15],[3,9,10],[9,10,12],[0,10,14],[0,6,14],[4,6,11],[11,14,15],[6,8,9],[8,13,14],[0,8,9],[2,7,13],[2,6,8],[0,5,10],[7,10,12],[2,4,10],[4,11,13],[3,6,7],[4,5,11],[2,5,9],[1,7,10],[2,9,15],[6,9,11],[0,3,7],[9,10,12],[4,13,15],[0,7,11],[1,5,14],[0,8,12],[5,8,13],[8,10,11],[0,13,14],[2,3,13],[3,9,11],[2,5,12],[3,6,11],[4,11,14],[1,6,13],[2,9,14],[5,7,14],[5,7,14],[4,8,13],[8,13,15],[7,11,15],[1,2,9],[1,10,12],[1,4,5],[4,6,11],[0,6,12],[1,3,4],[5,7,15],[2,6,12],[6,7,10],[0,1,13],[2,7,11],[5,6,12],[2,3,6],[2,3,11],[5,8,13],[1,3,6],[2,4,13],[2,8,10],[5,11,14],[4,5,6],[1,5,13],[1,5,14],[1,9,15],[1,4,8],[1,2,5],[1,13,15],[2,10,12],[2,11,14],[0,2,8],[2,10,11],[3,10,11],[0,11,15],[5,6,8],[0,3,11],[5,13,14],[4,10,14],[7,10,15],[5,6,11],[8,12,14],[4,10,13],[1,2,12],[1,10,13],[9,13,15],[4,8,15],[7,11,13],[3,10,12],[3,10,14],[0,2,3],[0,1,12],[13,14,15],[1,2,7],[0,11,15],[2,8,9],[0,6,14],[4,7,9],[1,9,13],[1,9,10],[5,11,14],[6,10,12],[3,5,10],[0,5,8],[7,8,15],[0,7,12],[1,7,9],[8,10,14],[5,12,13],[3,5,10],[0,5,15],[0,6,14],[2,11,14],[1,2,8],[7,11,14],[6,9,12],[7,10,15],[4,8,10],[4,14,15],[9,10,14],[1,3,8],[2,8,14],[0,7,14]]]
def setup_inputs(rng):
    rt = (0.75 * rng.standard_normal((128, 1), dtype=np.float32) + rng.standard_normal((128, N), dtype=np.float32) / 2).astype(ml_dtypes.bfloat16)
    rm = np.zeros((N, N, TOK), np.float32)
    for r in range(N):
        for t in range(TOK): rm[r, ROUTE[r][t], t] = 1.0
    return {"x": rng.standard_normal((N, 128, TOK), dtype=np.float32).astype(ml_dtypes.bfloat16), "rt": np.broadcast_to(rt, (N, 128, N)).copy(), "rm": rm.astype(ml_dtypes.bfloat16), "w": rng.standard_normal((N, 128, 128), dtype=np.float32).astype(ml_dtypes.bfloat16)}
def setup_inputs_big(rng):
    d = setup_inputs(rng)
    for k in ("x", "w"): d[k] = (d[k].astype(np.float32) * 1024.0).astype(d[k].dtype)
    return d
def setup_inputs_small(rng):
    d = setup_inputs(rng)
    for k in ("x", "w"): d[k] = (d[k].astype(np.float32) * (1 / 1024.0)).astype(d[k].dtype)
    return d
def setup_inputs_apart(rng):
    d = setup_inputs(rng)
    f = (10.0 ** rng.permutation(np.linspace(-1.5, 1.5, N))).astype(np.float32).reshape(N, 1, 1)
    for k in ("x",): d[k] = (d[k].astype(np.float32) * f).astype(d[k].dtype)
    return d
def setup_inputs_lure(rng):
    d = setup_inputs(rng); x = d["x"].astype(np.float32) * 1024; rt = d["rt"][0].astype(np.float32)
    for r in range(N):
        for t in range(TOK):
            u = int(rng.choice([e for e in range(N) if e not in ROUTE[r][t]]))
            x[r][:, t] += 2097152 * (rt[:, u] - rt[:, ROUTE[r][t][0]])
    d["x"] = x.astype(d["x"].dtype)
    return d
def reference(x, rt, rm, w):
    X, RT, W = x.astype(np.float64), rt.astype(np.float64), w.astype(np.float64)
    y = np.zeros((N, 128, TOK))
    for r in range(N):
        sc = RT[r].T @ X[r]
        for t in range(TOK):
            ex = ROUTE[r][t]; g = np.exp(sc[ex, t] - sc[ex, t].max()); g = g / g.sum()
            y[r][:, t] = sum(g[i] * (W[e].T @ X[r][:, t]) for i, e in enumerate(ex))
    return {"y": y.astype(ml_dtypes.bfloat16)}

from concourse.bass import DstId, RemoteDMATransfer
from concourse.mybir import AluOpType, AxisListType, ActivationFunctionType

BF, F32 = "bfloat16", "float32"
SCRATCH = {
    "land": ("dram", [16, 128, 128], BF),
    "W0": ("sbuf", [128, 512], BF), "W1": ("sbuf", [128, 512], BF),
    "W2": ("sbuf", [128, 512], BF), "W3": ("sbuf", [128, 512], BF),
    "xs": ("sbuf", [128, 256], BF), "Xr": ("sbuf", [128, 1024], BF),
    "rts": ("sbuf", [128, 16], BF), "rms": ("sbuf", [128, 256], BF),
    "ones": ("sbuf", [128, 128], BF), "ident": ("sbuf", [128, 128], BF),
    "zer": ("sbuf", [128, 512], BF), "onesS": ("sbuf", [128, 512], BF), "sel": ("sbuf", [128, 512], BF),
    "cap": ("sbuf", [128, 32], F32), "msk": ("sbuf", [128, 32], F32), "ex": ("sbuf", [128, 32], F32),
    "negm": ("sbuf", [128, 4], F32), "ssum": ("sbuf", [128, 4], F32), "rs": ("sbuf", [128, 4], F32),
    "gT": ("sbuf", [128, 32], BF), "gs": ("sbuf", [128, 256], BF),
    "R": ("sbuf", [128, 4096], BF), "ys": ("sbuf", [128, 256], BF),
    "p_rm": ("psum", [128, 512], F32), "p_s": ("psum", [128, 512], F32), "p_g": ("psum", [128, 512], F32),
    "pG0": ("psum", [128, 512], F32), "pG1": ("psum", [128, 512], F32),
    "pG2": ("psum", [128, 512], F32), "pG3": ("psum", [128, 512], F32),
    "p_y": ("psum", [128, 512], F32),
}
SEMAPHORES = ["v", "a", "p", "gq", "s_w", "s_x", "s_rm", "s_xr", "wl0", "wl1", "f0", "f1", "loc", "out"] + \
             ["a%d" % i for i in range(8)]
BIG = 5e28


def rank_program(g, core, T, topo):
    r = T.rank_of(core)
    if r is None:
        return
    S, cores, n = T.sem, T.cores, len(T.cores)
    A, ACT = AluOpType, ActivationFunctionType
    partner = [q for q in range(n) if q != r and topo.chip(cores[q]) == topo.chip(core)][0]
    mine = [q for q in range(n) if topo.die(cores[q]) == topo.die(core)]
    pos = mine.index(r)
    gi, i0 = pos // 4, pos % 4
    order = [mine[4 * gi + (i0 + k) % 4] for k in range(1, 4)] + [mine[4 * (1 - gi) + (i0 + k) % 4] for k in range(4)]
    g_own, g_oth = mine[4 * gi] // 4, mine[4 * (1 - gi)] // 4
    theirs = [q for q in range(n) if q not in mine]
    pp = theirs.index(partner) // 4
    g_f0, g_f1 = theirs[4 * pp] // 4, theirs[4 * (1 - pp)] // 4
    groups = [g_own, g_oth, g_f0, g_f1]
    ready = [S.wl0, S.wl1, S.f0, S.f1]
    W = [T.W0, T.W1, T.W2, T.W3]
    pG = [T.pG0, T.pG1, T.pG2, T.pG3]
    cnt = {"v": 0, "a": 0, "p": 0, "gq": 0}

    def done(instr, q):
        instr.then_inc(S[q], 1)
        cnt[q] += 1
        return cnt[q]

    V, P, SC, SY = g.vector, g.tensor, g.scalar, g.sync

    SY.dma_start(T.land[r], T.w[:]).then_inc(S.s_w, 16)
    SC.dma_start(T.xs[:], T.x[:]).then_inc(S.s_x, 16)
    SC.dma_start(T.rts[:], T.rt[:]).then_inc(S.s_x, 16)
    SC.dma_start(T.rms[0:16, :], T.rm[:]).then_inc(S.s_rm, 16)
    for i in range(4):
        SY.dma_start(T.Xr[32 * i:32 * i + 32, :], T.x[:]).then_inc(S.s_xr, 16)

    v_ones = done(V.memset(T.ones[:], 1.0), "v")
    v_zer = done(V.memset(T.zer[0:16, :], 0.0), "v")
    SC.wait_ge(S.v, v_zer)
    a_ones = done(SC.activation(T.onesS[0:16, :], T.zer[0:16, :], ACT.Exp), "a")
    g.wait_ge(S.v, v_ones)
    g_id = done(g.affine_select(T.ident[:], T.ones[:], [[-1, 128]], A.is_equal, 0.0, 0, 1), "gq")

    off = topo.mask(core, cores[order[0]])
    for q in order:
        off &= topo.mask(core, cores[q])
    ids = []
    for q in order:
        rid, pid, _se = topo.addr(cores[q])
        ids.append(DstId(rid=rid, pnc=pid))
    g.wait_ge(S.s_w, 16)
    g.remote_dma_fused([RemoteDMATransfer(dst_ids=ids, dma_engine_mask=off, remote_sem=S["a%d" % pos],
                                          srcs=[T.land[r]], dsts=[T.land[r] for _q in order], alu_op=0)],
                       local_sem=S.loc)
    n_loc = bin(off).count("1")
    g.wait_ge(S.a, a_ones)
    g_sel = done(g.affine_select(T.sel[0:16, :], T.onesS[0:16, :], [[-1, 16], [0, 32]], A.is_equal, 0.0, 0, 1), "gq")

    SY.wait_ge(S.s_w, 16)
    for k, (G, half) in enumerate(((g_own, gi), (g_oth, 1 - gi))):
        for j in range(4):
            if 4 * half + j != pos:
                SY.wait_ge(S["a%d" % (4 * half + j)], n_loc)
        SY.dma_start(W[G][:], T.land[4 * G:4 * G + 4]).then_inc(ready[k], 16)

    prid, ppid, _se = topo.addr(cores[partner])
    on = topo.mask(core, cores[partner])
    for k, G in enumerate((g_own, g_oth)):
        g.wait_ge(ready[k], 16)
        g.remote_dma(W[G][:], W[G][:], (S.f0, S.f1)[k], S.loc, ppid, prid, on)
        n_loc += bin(on).count("1")
    n_on = bin(on).count("1")

    P.wait_ge(S.s_rm, 16)
    P.wait_ge(S.gq, g_id)
    done(P.matmul(T.p_rm[:, 0:16], T.rms[0:16, 0:128], T.ident[0:16, 0:16], True, True), "p")
    p_rm = done(P.matmul(T.p_rm[:, 16:32], T.rms[0:16, 128:256], T.ident[0:16, 0:16], True, True), "p")
    V.wait_ge(S.p, p_rm)
    v_cap = done(V.tensor_scalar(T.cap[:], T.p_rm[:, 0:32], 2 * BIG, BIG, A.mult, A.subtract), "v")
    P.wait_ge(S.s_x, 32)
    done(P.matmul(T.p_s[:, 0:16], T.xs[:, 0:128], T.rts[:], True, True), "p")
    p_s = done(P.matmul(T.p_s[:, 16:32], T.xs[:, 128:256], T.rts[:], True, True), "p")
    V.wait_ge(S.p, p_s)
    V.wait_ge(S.v, v_cap)
    v_m = done(V.tensor_tensor(T.msk[:], T.p_s[:, 0:32], T.cap[:], A.min), "v")
    V.wait_ge(S.v, v_m)
    a_e = 0
    for b in range(2):
        v_r = done(V.tensor_reduce(T.negm[:, b:b + 1], T.msk[:, 16 * b:16 * b + 16], AxisListType.X, A.max,
                                   negate=True), "v")
        SC.wait_ge(S.v, v_r)
        a_e = done(SC.activation(T.ex[:, 16 * b:16 * b + 16], T.msk[:, 16 * b:16 * b + 16], ACT.Exp,
                                 bias=T.negm[:, b:b + 1], scale=1.0, accum_out=T.ssum[:, b:b + 1]), "a")
    V.wait_ge(S.a, a_e)
    v_rs = done(V.reciprocal(T.rs[:, 0:2], T.ssum[:, 0:2]), "v")
    V.wait_ge(S.v, v_rs)
    v_g = 0
    for b in range(2):
        v_g = done(V.tensor_scalar(T.gT[:, 16 * b:16 * b + 16], T.ex[:, 16 * b:16 * b + 16], T.rs[:, b:b + 1], None,
                                   A.mult), "v")
    P.wait_ge(S.v, v_g)
    done(P.matmul(T.p_g[0:16, 0:128], T.gT[:, 0:16], T.ident[:], True, True), "p")
    p_g = done(P.matmul(T.p_g[0:16, 128:256], T.gT[:, 16:32], T.ident[:], True, True), "p")
    V.wait_ge(S.p, p_g)
    v_gs = done(V.tensor_copy(T.gs[0:16, :], T.p_g[0:16, 0:256]), "v")

    P.wait_ge(S.v, v_gs)
    P.wait_ge(S.gq, g_sel)
    pGd = [done(P.matmul(pG[G][:, 0:256], T.sel[0:16, 128 * G:128 * G + 128], T.gs[0:16, :], True, True), "p")
           for G in groups]
    V.wait_ge(S.s_xr, 64)
    vR = []
    for k, G in enumerate(groups):
        V.wait_ge(S.p, pGd[k])
        for s in range(4):
            c = (4 * k + s) * 256
            vR.append(done(V.tensor_tensor(T.R[:, c:c + 256], pG[G][:, 0:256], T.Xr[:, 256 * s:256 * s + 256],
                                           A.mult), "v"))
    p_y = 0
    for k, G in enumerate(groups):
        P.wait_ge(ready[k], 16 if k < 2 else n_on)
        for s in range(4):
            j = 4 * k + s
            P.wait_ge(S.v, vR[j])
            p_y = done(P.matmul(T.p_y[:, 0:256], W[G][:, 128 * s:128 * s + 128], T.R[:, 256 * j:256 * j + 256],
                                j == 0, j == 15), "p")
    V.wait_ge(S.p, p_y)
    v_y = done(V.tensor_copy(T.ys[:], T.p_y[:, 0:256]), "v")
    SY.wait_ge(S.v, v_y)
    SY.dma_start(T.y[:], T.ys[:]).then_inc(S.out, 16)
    SY.wait_ge(S.out, 16)
    g.wait_ge(S.loc, n_loc)
